import numpy as np
import ml_dtypes


def mxq(x, axis, fmt="e4m3"):
    dtype, down = {"e4m3": (ml_dtypes.float8_e4m3fn, 7), "e5m2": (ml_dtypes.float8_e5m2, 14)}[fmt]
    v = np.moveaxis(np.asarray(x, np.float32).astype(ml_dtypes.bfloat16).astype(np.float64), axis, -1)
    blocks = v.reshape(v.shape[:-1] + (-1, 32))
    amax = np.abs(blocks).max(-1, keepdims=True)
    byte = np.maximum(np.where(amax > 0, np.frexp(amax)[1] - 1 + 127, 0) - down, 1)
    scale = np.exp2(byte - 127.0)
    codes = (blocks / scale).astype(np.float32).astype(dtype).astype(np.float64)
    return np.moveaxis((codes * scale).reshape(v.shape), -1, axis)


WIDE = False


def mx_kscale(k):
    if not WIDE:
        return np.ones(k)
    levels = np.array([10, -10, 5, -5, 0])
    if k % 512:
        return np.exp2(np.random.permutation(np.resize(levels, k // 32))).repeat(32)
    a = np.empty((k // 512, 16))
    for p in range(k // 512):
        a[p, :8] = np.random.permutation(np.resize(levels, 8))
        for g in range(8):
            far = levels[np.abs(levels - a[p, g]) >= 10]
            a[p, g + 8] = far[np.random.randint(len(far))]
    return np.exp2(a.ravel()).repeat(32)


def f64(x):
    return np.asarray(x).astype(np.float64)


def striped(idx):
    return np.tile(np.asarray(idx).reshape(-1, 16).T, (8, 1)).astype(np.uint16)


def unstriped(offs):
    return offs[:16].T.reshape(-1).astype(np.int64)


E2M1 = np.array([0.0, 0.5, 1.0, 1.5, 2.0, 3.0, 4.0, 6.0, -0.0, -0.5, -1.0, -1.5, -2.0, -3.0, -4.0, -6.0])


def pack_weight(w, fmt):
    k, n = w.shape
    w = f64(np.asarray(w, np.float32).astype(ml_dtypes.bfloat16)).reshape(k // 32, 32, n)
    amax = np.abs(w).max(1)
    if fmt == "e4m3":
        byte = np.frexp(amax)[1] - 1 + 127 - 7
    else:
        mant, ex = np.frexp(amax / 6.0)
        byte = np.where(mant > 0.5, ex, ex - 1) + 127
    byte = np.clip(np.where(amax > 0, byte, 1), 1, 254)
    scaled = (w * np.exp2(127.0 - byte)[:, None, :]).reshape(k, n).astype(np.float32)
    by_word = np.ascontiguousarray(scaled.reshape(k // 512, 128, 4, n).transpose(0, 1, 3, 2))
    if fmt == "e4m3":
        words = by_word.astype(ml_dtypes.float8_e4m3fn).view(np.uint8)
    else:
        c = by_word.astype(ml_dtypes.float4_e2m1fn).view(np.uint8) & 0xF
        words = (c[..., 0::2] | (c[..., 1::2] << 4)).reshape(k // 512, 128, 2 * n)
    return np.ascontiguousarray(words), np.ascontiguousarray(byte.astype(np.uint8).reshape(k // 512, 16, n))


def unpack_weight(words, scales, fmt):
    g, _, n = scales.shape
    words = np.ascontiguousarray(words).reshape(g, 128, n, -1)
    if fmt == "e4m3":
        vals = words.view(ml_dtypes.float8_e4m3fn).astype(np.float64)
    else:
        nib = np.empty((g, 128, n, 4), np.uint8)
        nib[..., 0::2] = words & 0xF
        nib[..., 1::2] = words >> 4
        vals = E2M1[nib]
    vals = vals * np.repeat(np.exp2(scales.astype(np.float64) - 127.0), 8, axis=1)[..., None]
    return vals.transpose(0, 1, 3, 2).reshape(g * 512, n)


def sigmoid(v):
    return 1.0 / (1.0 + np.exp(-v))


def bf(x):
    return np.asarray(x, np.float32).astype(ml_dtypes.bfloat16)


def planes(Y):
    r, m = Y.shape
    b = f64(bf(Y)).reshape(r // 32, 32, m)
    amax = np.abs(b).max(1)
    byte = np.clip(np.where(amax > 0, np.frexp(amax)[1] - 1 + 127 - 7, 1), 1, 254)
    codes = (b * np.exp2(127.0 - byte)[:, None, :]).reshape(r, m).astype(np.float32).astype(ml_dtypes.float8_e4m3fn).view(np.uint8)
    words = codes.reshape(r // 512, 128, 4, m).transpose(0, 1, 3, 2)
    return np.ascontiguousarray(words), np.ascontiguousarray(byte.astype(np.uint8).reshape(r // 512, 16, m))


K, R, F, T, J = 512, 512, 512, 2048, 256


def setup_inputs():
    n = np.random.standard_normal
    idx = np.random.permutation(T)[:J]
    fk = mx_kscale(K)
    fr = mx_kscale(R)
    tabp = pack_weight(n((K, T)) / fk[:, None], "e2m1")
    dtabp = pack_weight(n((K, T)) / fk[:, None], "e2m1")
    return {
        "tab_words": tabp[0],
        "tab_scales": tabp[1],
        "dtab_words": dtabp[0],
        "dtab_scales": dtabp[1],
        "w1": (n((K, R)) * 1 / np.sqrt(K) * fk[:, None]).astype(np.float32),
        "gain": (np.random.uniform(0.5, 1.5, (R, 1))).astype(np.float32),
        "rs": (np.random.uniform(0.5, 2.0, (R, 1)) * fr[:, None]).astype(np.float32),
        "wor": (n((R, F)) * 1 / np.sqrt(R) / fr[:, None]).astype(np.float32),
        "res": (n((F, J)) * 0.5).astype(np.float32),
        "offs": striped(idx),
    }


def reference(tab_words, tab_scales, dtab_words, dtab_scales, w1, gain, rs, wor, res, offs):
    idx = unstriped(offs)
    tabu = unpack_weight(tab_words, tab_scales, "e2m1")
    dtabu = unpack_weight(dtab_words, dtab_scales, "e2m1")
    w1q = mxq(f64(w1), 0, "e4m3")
    tabidxg = tabu[:, idx]
    a = w1q.T @ tabidxg
    dtabidxg = dtabu[:, idx]
    ta = w1q.T @ dtabidxg
    n1 = np.sqrt(np.mean(np.square(a), axis=1, keepdims=True) + 0.01)
    s = a / n1 * f64(gain)
    tn1 = np.mean(ta * a * 2.0, axis=1, keepdims=True) * 0.5 / n1
    ts = (ta - tn1 * a / n1) / n1 * f64(gain)
    tu1 = ts * sigmoid(s) + ts * sigmoid(s) * (1.0 - sigmoid(s)) * s
    fo1 = tu1 * f64(rs)
    worq = mxq(f64(wor), 0, "e4m3")
    fo1q = mxq(fo1, 0, "e4m3")
    yo = worq.T @ fo1q
    y = yo + f64(res)
    words, scales = planes(y)
    return y, words, scales

@@ -1,0 +1,226 @@
+from contextlib import ExitStack
+
+import concourse.mybir as mybir
+
+K, R, F, T, J = 512, 512, 512, 2048, 256
+FLOPS = 2 * (2 * K * R * J + R * F * J)
+
+F32 = mybir.dt.float32
+BF16 = mybir.dt.bfloat16
+I32 = mybir.dt.int32
+U32 = mybir.dt.uint32
+U16 = mybir.dt.uint16
+U8 = mybir.dt.uint8
+FP8X4 = mybir.dt.float8_e4m3fn_x4
+FP4X4 = mybir.dt.float4_e2m1fn_x4
+ACT = mybir.ActivationFunctionType
+ALU = mybir.AluOpType
+
+P = 128
+PACK = 4
+HALF = J // 2
+EPS = 0.01
+
+
+def tile_attend_tcslotnorm_o_pl_kernel(
+    tc, tab_words, tab_scales, dtab_words, dtab_scales, w1, gain, rs, wor, res, offs, out_0, out_1, out_2
+):
+    nc = tc.nc
+    with ExitStack() as ctx:
+        sb = ctx.enter_context(tc.tile_pool(name="sb", bufs=1))
+        ps = ctx.enter_context(tc.psum_pool(name="ps", bufs=1))
+
+        def tile(name, shape, dtype, tag=None):
+            return sb.tile(shape, dtype, name=name, tag=tag or name, align_bytes=64)
+
+        offsets = sb.tile([P, J // 16], U16, name="offsets")
+        tab_w = tile("tab_w", [P, T], U16)
+        tab_s = tile("tab_s", [P, T], U8)
+        dtab_s = tile("dtab_s", [P, T], U8)
+        gain_sb = tile("gain_sb", [P, PACK], F32)
+        rs_sb = tile("rs_sb", [P, PACK], F32)
+        exponent = tile("exponent", [P, PACK], F32)
+        warm = tile("warm", [P, 1], F32)
+
+        nc.vector.memset(tab_s[:].bitcast(I32), 0)
+        nc.vector.memset(exponent[:], -0.5)
+        nc.vector.memset(dtab_s[:].bitcast(I32), 0)
+        nc.scalar.activation(warm[:], exponent[:, 0:1], ACT.Silu)
+        nc.gpsimd.dma_start(out=gain_sb[:], in_=gain.rearrange("(p t) o -> p (t o)", t=PACK))
+        nc.gpsimd.dma_start(out=rs_sb[:], in_=rs.rearrange("(p t) o -> p (t o)", t=PACK))
+
+        def load_scales(dst, src):
+            for q in range(4):
+                nc.sync.dma_start(out=dst[32 * q : 32 * q + 4, :].bitcast(I32), in_=src[0, 4 * q : 4 * q + 4, :].bitcast(I32))
+
+        def load_weight(dst, src, h):
+            rows = src.rearrange("(p j) c -> p j c", j=PACK)
+            nc.sync.dma_start(out=dst[h][:], in_=rows[:, :, h * 256 : (h + 1) * 256])
+
+        w1_raw = [tile("w1_raw%d" % h, [P, PACK, R // 2], F32) for h in range(2)]
+        dtab_w = tile("dtab_w", [P, T], U16)
+        nc.sync.dma_start(offsets[:], offs)
+        load_weight(w1_raw, w1, 0)
+        load_scales(tab_s, tab_scales)
+        load_weight(w1_raw, w1, 1)
+        nc.sync.dma_start(out=tab_w[:].bitcast(I32), in_=tab_words[0].bitcast(I32))
+        nc.sync.dma_start(out=dtab_w[:].bitcast(I32), in_=dtab_words[0].bitcast(I32))
+        load_scales(dtab_s, dtab_scales)
+        wor_raw = [tile("wor_raw%d" % h, [P, PACK, F // 2], F32) for h in range(2)]
+        load_weight(wor_raw, wor, 0)
+        load_weight(wor_raw, wor, 1)
+        res_sb = tile("res_sb", [P, PACK, J], F32)
+        nc.sync.dma_start(out=res_sb[:], in_=res.rearrange("(p t) j -> p t j", t=PACK))
+
+        root = float(J) ** 0.5
+        coef = tile("coef", [P, 4, PACK], F32)
+        nc.gpsimd.tensor_scalar(coef[:, 0, :], gain_sb[:], 0.5 * root, 0.0, ALU.mult, ALU.add)
+        nc.gpsimd.tensor_scalar(coef[:, 1, :], gain_sb[:], -root, 0.0, ALU.mult, ALU.add)
+        nc.gpsimd.tensor_tensor(coef[:, 2, :], coef[:, 0, :], rs_sb[:], ALU.mult)
+        nc.gpsimd.tensor_scalar(coef[:, 3, :], coef[:, 2, :], -1.0, 0.0, ALU.mult, ALU.add)
+
+        def gather(name, window, dtype):
+            picked = tile(name, [P, J], dtype)
+            nc.vector.tensor_copy(picked[:], window[:].indirect(offsets[:]))
+            return picked
+
+        def deal(copy, grouped, raw, h, lo=0, hi=64):
+            copy(
+                grouped[:, :, h * 64 + lo : h * 64 + hi, :].rearrange("p t m j -> p m j t"),
+                raw[h][:, :, PACK * lo : PACK * hi].rearrange("p j (m t) -> p m j t", t=PACK),
+            )
+
+        x_s = gather("x_s", tab_s, U8)
+
+        w1_bf = tile("w1_bf", [P, PACK, P, PACK], BF16)
+        w1_q = tile("w1_q", [P, PACK, P], U32)
+        w1_s = tile("w1_s", [P, PACK, P], U8)
+        deal(nc.scalar.copy, w1_bf, w1_raw, 0)
+        deal(nc.vector.tensor_copy, w1_bf, w1_raw, 1, 0, 44)
+        deal(nc.scalar.copy, w1_bf, w1_raw, 1, 44, 64)
+        for t in range(PACK):
+            nc.vector.quantize_mx(
+                out=w1_q[:, t, :].bitcast(FP8X4), scales=w1_s[:, t, :], in_=w1_bf[:, t, :, :].rearrange("p m j -> p (m j)")
+            )
+
+        def first_layer(name, words, scales):
+            banks = [ps.tile([P, 2, J], F32, name="%s%d" % (name, b)) for b in range(2)]
+            for t in range(PACK):
+                nc.tensor.matmul_mx(
+                    out=banks[t // 2][:, t % 2, :],
+                    lhsT=w1_q[:, t, :].bitcast(FP8X4),
+                    lhsT_scale=w1_s[:, t, :],
+                    rhs=words[:].bitcast(FP4X4),
+                    rhs_scale=scales[:],
+                    start=True,
+                    stop=True,
+                )
+            return banks
+
+        x_w = gather("x_w", tab_w, U16)
+        a_ps = first_layer("a_ps", x_w, x_s)
+        dx_w = gather("dx_w", dtab_w, U16)
+        dx_s = gather("dx_s", dtab_s, U8)
+        ta_ps = first_layer("ta_ps", dx_w, dx_s)
+
+        a_sb = tile("a_sb", [P, PACK, J], F32)
+        th = tile("th", [P, PACK, J], F32)
+        ms = tile("ms", [P, PACK, J], F32)
+        u = tile("u", [P, PACK, J], F32)
+        left = tile("left", [P, PACK, J], F32)
+        right = tile("right", [P, PACK, J], F32)
+        ssq = tile("ssq", [P, PACK], F32)
+        msq = tile("msq", [P, PACK], F32)
+        rinv = tile("rinv", [P, PACK], F32)
+        scaled = tile("scaled", [P, 4, PACK], F32)
+        qinv = tile("qinv", [P, PACK], F32, tag="dtab_s")
+        proj = tile("proj", [P, PACK], F32)
+
+        for b in range(2):
+            pair = slice(2 * b, 2 * b + 2)
+            for t in range(2 * b, 2 * b + 2):
+                nc.scalar.activation(th[:, t, :], a_ps[b][:, t % 2, :], ACT.Square, accum_out=ssq[:, t : t + 1])
+            nc.gpsimd.tensor_scalar(msq[:, pair], ssq[:, pair], EPS * J, 1.0, ALU.add, ALU.mult)
+            nc.gpsimd.tensor_tensor(rinv[:, pair], msq[:, pair], exponent[:, pair], ALU.pow)
+            nc.gpsimd.tensor_tensor(
+                scaled[:, :, pair], coef[:, :, pair], rinv[:, pair].unsqueeze(1).to_broadcast([P, 4, 2]), ALU.mult
+            )
+            nc.scalar.copy(a_sb[:, pair, :], a_ps[b][:])
+
+        for b in range(2):
+            pair = slice(2 * b, 2 * b + 2)
+            nc.vector.reciprocal(qinv[:, pair], msq[:, pair])
+            for t in range(2 * b, 2 * b + 2):
+                nc.vector.scalar_tensor_tensor(
+                    u[:, t, :], ta_ps[b][:, t % 2, :], qinv[:, t : t + 1], a_sb[:, t, :], ALU.mult, ALU.mult, accum_out=proj[:, t : t + 1]
+                )
+            for t in range(2 * b, 2 * b + 2):
+                nc.vector.scalar_tensor_tensor(
+                    u[:, t, :], a_sb[:, t, :], proj[:, t : t + 1], ta_ps[b][:, t % 2, :], ALU.mult, ALU.subtract
+                )
+
+        for b in range(2):
+            for t in range(2 * b, 2 * b + 2):
+                nc.scalar.activation(th[:, t, :], a_sb[:, t, :], ACT.Tanh, scale=scaled[:, 0, t : t + 1])
+            for t in range(2 * b, 2 * b + 2):
+                nc.scalar.activation(ms[:, t, :], a_sb[:, t, :], ACT.Silu, scale=scaled[:, 1, t : t + 1])
+            for t in range(2 * b, 2 * b + 2):
+                nc.scalar.activation(
+                    right[:, t, :], ms[:, t, :], ACT.Identity, scale=scaled[:, 2, t : t + 1], bias=scaled[:, 3, t : t + 1]
+                )
+
+        wor_bf = tile("wor_bf", [P, PACK, P, PACK], BF16)
+        wor_q = tile("wor_q", [P, PACK * P], U32)
+        wor_s = tile("wor_s", [P, PACK * P], U8)
+        for b in range(2):
+            pair = slice(2 * b, 2 * b + 2)
+            nc.vector.scalar_tensor_tensor(left[:, pair, :], th[:, pair, :], 1.0, u[:, pair, :], ALU.add, ALU.mult)
+        deal(nc.vector.tensor_copy, wor_bf, wor_raw, 0)
+        deal(nc.vector.tensor_copy, wor_bf, wor_raw, 1, 0, 32)
+        deal(nc.scalar.copy, wor_bf, wor_raw, 1, 32, 64)
+        nc.vector.quantize_mx(out=wor_q[:].bitcast(FP8X4), scales=wor_s[:], in_=wor_bf[:].rearrange("p t m j -> p (t m j)"))
+
+        def by_fours(ap):
+            return ap.rearrange("p t (c i) -> p c t i", i=4)
+
+        def woven(ap):
+            return ap.rearrange("p (c i) t -> p c t i", i=4)
+
+        y_q = tile("y_q", [P, J], U32)
+        y_s = tile("y_s", [P, J], U8)
+        y_rows = out_0.rearrange("(p t) j -> p t j", t=PACK)
+        y_ps = []
+        for h in range(2):
+            cols = slice(h * HALF, (h + 1) * HALF)
+            fo_bf = tile("fo_bf%d" % h, [P, HALF, PACK], BF16)
+            fo_q = tile("fo_q%d" % h, [P, HALF], U32)
+            fo_s = tile("fo_s%d" % h, [P, HALF], U8)
+            nc.vector.tensor_tensor(woven(fo_bf[:]), by_fours(left[:, :, cols]), by_fours(right[:, :, cols]), ALU.mult)
+            nc.vector.quantize_mx(out=fo_q[:].bitcast(FP8X4), scales=fo_s[:], in_=fo_bf[:].rearrange("p j t -> p (j t)"))
+            bank = ps.tile([P, PACK, HALF], F32, name="y_ps%d" % h)
+            for t in range(PACK):
+                nc.tensor.matmul_mx(
+                    out=bank[:, t, :],
+                    lhsT=wor_q[:, t * P : (t + 1) * P].bitcast(FP8X4),
+                    lhsT_scale=wor_s[:, t * P : (t + 1) * P],
+                    rhs=fo_q[:].bitcast(FP8X4),
+                    rhs_scale=fo_s[:],
+                    start=True,
+                    stop=True,
+                )
+            y_ps.append(bank)
+        for h in range(2):
+            cols = slice(h * HALF, (h + 1) * HALF)
+            y = tile("y%d" % h, [P, PACK, HALF], F32)
+            y_bf = tile("y_bf%d" % h, [P, HALF, PACK], BF16)
+            nc.vector.tensor_tensor(y[:], y_ps[h][:], res_sb[:, :, cols], ALU.add)
+            nc.sync.dma_start(out=y_rows[:, :, cols], in_=y[:])
+            copy = nc.scalar.copy if h == 0 else nc.vector.tensor_copy
+            copy(woven(y_bf[:]), by_fours(y[:]))
+            nc.vector.quantize_mx(
+                out=y_q[:, cols].bitcast(FP8X4), scales=y_s[:, cols], in_=y_bf[:].rearrange("p j t -> p (j t)")
+            )
+        nc.sync.dma_start(out=out_1[0].rearrange("p c r -> p (c r)").bitcast(I32), in_=y_q[:].bitcast(I32))
+        for q in range(4):
+            queue = nc.scalar if q % 2 == 0 else nc.sync
+            queue.dma_start(out=out_2[0, 4 * q : 4 * q + 4, :].bitcast(I32), in_=y_s[32 * q : 32 * q + 4, :].bitcast(I32))

@@ -50,8 +50,8 @@ def tile_attend_tcslotnorm_o_pl_kernel(
         nc.gpsimd.dma_start(out=rs_sb[:], in_=rs.rearrange("(p t) o -> p (t o)", t=PACK))
 
         def load_scales(dst, src):
-            for q in range(4):
-                nc.sync.dma_start(out=dst[32 * q : 32 * q + 4, :].bitcast(I32), in_=src[0, 4 * q : 4 * q + 4, :].bitcast(I32))
+            for r in range(4):
+                nc.sync.dma_start(out=dst[r:P:32, :].bitcast(I32), in_=src[0, r:16:4, :].bitcast(I32))
 
         def load_weight(dst, src, h):
             rows = src.rearrange("(p j) c -> p j c", j=PACK)
@@ -59,8 +59,8 @@ def tile_attend_tcslotnorm_o_pl_kernel(
 
         w1_raw = [tile("w1_raw%d" % h, [P, PACK, R // 2], F32) for h in range(2)]
         dtab_w = tile("dtab_w", [P, T], U16)
-        nc.sync.dma_start(offsets[:], offs)
         load_weight(w1_raw, w1, 0)
+        nc.sync.dma_start(offsets[:], offs)
         load_scales(tab_s, tab_scales)
         load_weight(w1_raw, w1, 1)
         nc.sync.dma_start(out=tab_w[:].bitcast(I32), in_=tab_words[0].bitcast(I32))
@@ -86,8 +86,8 @@ def tile_attend_tcslotnorm_o_pl_kernel(
 
         def deal(copy, grouped, raw, h, lo=0, hi=64):
             copy(
-                grouped[:, :, h * 64 + lo : h * 64 + hi, :].rearrange("p t m j -> p m j t"),
-                raw[h][:, :, PACK * lo : PACK * hi].rearrange("p j (m t) -> p m j t", t=PACK),
+                grouped[:, :, h * 64 + lo : h * 64 + hi, :].rearrange("p t m j -> p m t j"),
+                raw[h][:, :, PACK * lo : PACK * hi].rearrange("p j (m t) -> p m t j", t=PACK),
             )
 
         x_s = gather("x_s", tab_s, U8)
@@ -104,10 +104,10 @@ def tile_attend_tcslotnorm_o_pl_kernel(
             )
 
         def first_layer(name, words, scales):
-            banks = [ps.tile([P, 2, J], F32, name="%s%d" % (name, b)) for b in range(2)]
+            banks = [ps.tile([P, J], F32, name="%s%d" % (name, t)) for t in range(PACK)]
             for t in range(PACK):
                 nc.tensor.matmul_mx(
-                    out=banks[t // 2][:, t % 2, :],
+                    out=banks[t][:],
                     lhsT=w1_q[:, t, :].bitcast(FP8X4),
                     lhsT_scale=w1_s[:, t, :],
                     rhs=words[:].bitcast(FP4X4),
@@ -133,30 +133,33 @@ def tile_attend_tcslotnorm_o_pl_kernel(
         msq = tile("msq", [P, PACK], F32)
         rinv = tile("rinv", [P, PACK], F32)
         scaled = tile("scaled", [P, 4, PACK], F32)
-        qinv = tile("qinv", [P, PACK], F32, tag="dtab_s")
         proj = tile("proj", [P, PACK], F32)
 
         for b in range(2):
             pair = slice(2 * b, 2 * b + 2)
             for t in range(2 * b, 2 * b + 2):
-                nc.scalar.activation(th[:, t, :], a_ps[b][:, t % 2, :], ACT.Square, accum_out=ssq[:, t : t + 1])
+                nc.scalar.activation(th[:, t, :], a_ps[t][:], ACT.Square, accum_out=ssq[:, t : t + 1])
             nc.gpsimd.tensor_scalar(msq[:, pair], ssq[:, pair], EPS * J, 1.0, ALU.add, ALU.mult)
             nc.gpsimd.tensor_tensor(rinv[:, pair], msq[:, pair], exponent[:, pair], ALU.pow)
             nc.gpsimd.tensor_tensor(
                 scaled[:, :, pair], coef[:, :, pair], rinv[:, pair].unsqueeze(1).to_broadcast([P, 4, 2]), ALU.mult
             )
-            nc.scalar.copy(a_sb[:, pair, :], a_ps[b][:])
+            for t in range(2 * b, 2 * b + 2):
+                nc.scalar.copy(a_sb[:, t, :], a_ps[t][:])
 
+        wor_bf = tile("wor_bf", [P, PACK, P, PACK], BF16)
+        deal(nc.vector.tensor_copy, wor_bf, wor_raw, 0)
+        qinv = tile("qinv", [P, PACK], F32, tag="wor_raw0")
         for b in range(2):
             pair = slice(2 * b, 2 * b + 2)
             nc.vector.reciprocal(qinv[:, pair], msq[:, pair])
             for t in range(2 * b, 2 * b + 2):
                 nc.vector.scalar_tensor_tensor(
-                    u[:, t, :], ta_ps[b][:, t % 2, :], qinv[:, t : t + 1], a_sb[:, t, :], ALU.mult, ALU.mult, accum_out=proj[:, t : t + 1]
+                    u[:, t, :], ta_ps[t][:], qinv[:, t : t + 1], a_sb[:, t, :], ALU.mult, ALU.mult, accum_out=proj[:, t : t + 1]
                 )
             for t in range(2 * b, 2 * b + 2):
                 nc.vector.scalar_tensor_tensor(
-                    u[:, t, :], a_sb[:, t, :], proj[:, t : t + 1], ta_ps[b][:, t % 2, :], ALU.mult, ALU.subtract
+                    u[:, t, :], a_sb[:, t, :], proj[:, t : t + 1], ta_ps[t][:], ALU.mult, ALU.subtract
                 )
 
         for b in range(2):
@@ -169,15 +172,13 @@ def tile_attend_tcslotnorm_o_pl_kernel(
                     right[:, t, :], ms[:, t, :], ACT.Identity, scale=scaled[:, 2, t : t + 1], bias=scaled[:, 3, t : t + 1]
                 )
 
-        wor_bf = tile("wor_bf", [P, PACK, P, PACK], BF16)
         wor_q = tile("wor_q", [P, PACK * P], U32)
         wor_s = tile("wor_s", [P, PACK * P], U8)
         for b in range(2):
             pair = slice(2 * b, 2 * b + 2)
             nc.vector.scalar_tensor_tensor(left[:, pair, :], th[:, pair, :], 1.0, u[:, pair, :], ALU.add, ALU.mult)
-        deal(nc.vector.tensor_copy, wor_bf, wor_raw, 0)
         deal(nc.vector.tensor_copy, wor_bf, wor_raw, 1, 0, 32)
-        deal(nc.scalar.copy, wor_bf, wor_raw, 1, 32, 64)
+        deal(nc.vector.tensor_copy, wor_bf, wor_raw, 1, 32, 64)
         nc.vector.quantize_mx(out=wor_q[:].bitcast(FP8X4), scales=wor_s[:], in_=wor_bf[:].rearrange("p t m j -> p (t m j)"))
 
         def by_fours(ap):
@@ -189,6 +190,7 @@ def tile_attend_tcslotnorm_o_pl_kernel(
         y_q = tile("y_q", [P, J], U32)
         y_s = tile("y_s", [P, J], U8)
         y_rows = out_0.rearrange("(p t) j -> p t j", t=PACK)
+        y_words = out_1[0].rearrange("p c r -> p (c r)").bitcast(I32)
         y_ps = []
         for h in range(2):
             cols = slice(h * HALF, (h + 1) * HALF)
@@ -197,7 +199,7 @@ def tile_attend_tcslotnorm_o_pl_kernel(
             fo_s = tile("fo_s%d" % h, [P, HALF], U8)
             nc.vector.tensor_tensor(woven(fo_bf[:]), by_fours(left[:, :, cols]), by_fours(right[:, :, cols]), ALU.mult)
             nc.vector.quantize_mx(out=fo_q[:].bitcast(FP8X4), scales=fo_s[:], in_=fo_bf[:].rearrange("p j t -> p (j t)"))
-            bank = ps.tile([P, PACK, HALF], F32, name="y_ps%d" % h)
+            bank = ps.tile([P, PACK, HALF], F32, name="y_ps%d" % h, tag="a_ps%d" % h)
             for t in range(PACK):
                 nc.tensor.matmul_mx(
                     out=bank[:, t, :],
@@ -213,14 +215,16 @@ def tile_attend_tcslotnorm_o_pl_kernel(
             cols = slice(h * HALF, (h + 1) * HALF)
             y = tile("y%d" % h, [P, PACK, HALF], F32)
             y_bf = tile("y_bf%d" % h, [P, HALF, PACK], BF16)
+            if h == 1:
+                nc.vector.tensor_tensor(woven(y_bf[:]), by_fours(y_ps[h][:]), by_fours(res_sb[:, :, cols]), ALU.add)
             nc.vector.tensor_tensor(y[:], y_ps[h][:], res_sb[:, :, cols], ALU.add)
             nc.sync.dma_start(out=y_rows[:, :, cols], in_=y[:])
-            copy = nc.scalar.copy if h == 0 else nc.vector.tensor_copy
-            copy(woven(y_bf[:]), by_fours(y[:]))
+            if h == 0:
+                nc.scalar.copy(woven(y_bf[:]), by_fours(y[:]))
             nc.vector.quantize_mx(
                 out=y_q[:, cols].bitcast(FP8X4), scales=y_s[:, cols], in_=y_bf[:].rearrange("p j t -> p (j t)")
             )
-        nc.sync.dma_start(out=out_1[0].rearrange("p c r -> p (c r)").bitcast(I32), in_=y_q[:].bitcast(I32))
-        for q in range(4):
-            queue = nc.scalar if q % 2 == 0 else nc.sync
-            queue.dma_start(out=out_2[0, 4 * q : 4 * q + 4, :].bitcast(I32), in_=y_s[32 * q : 32 * q + 4, :].bitcast(I32))
+            nc.scalar.dma_start(out=y_words[:, cols], in_=y_q[:, cols].bitcast(I32))
+        for r in range(4):
+            queue = nc.sync if r % 2 == 0 else nc.scalar
+            queue.dma_start(out=out_2[0, r:16:4, :].bitcast(I32), in_=y_s[r:P:32, :].bitcast(I32))

@@ -43,15 +43,13 @@ def tile_attend_tcslotnorm_o_pl_kernel(
         warm = tile("warm", [P, 1], F32)
 
         nc.vector.memset(tab_s[:].bitcast(I32), 0)
-        nc.vector.memset(exponent[:], -0.5)
         nc.vector.memset(dtab_s[:].bitcast(I32), 0)
-        nc.scalar.activation(warm[:], exponent[:, 0:1], ACT.Silu)
+        nc.vector.memset(exponent[:], -0.5)
         nc.gpsimd.dma_start(out=gain_sb[:], in_=gain.rearrange("(p t) o -> p (t o)", t=PACK))
         nc.gpsimd.dma_start(out=rs_sb[:], in_=rs.rearrange("(p t) o -> p (t o)", t=PACK))
 
         def load_scales(dst, src):
-            for r in range(4):
-                nc.sync.dma_start(out=dst[r:P:32, :].bitcast(I32), in_=src[0, r:16:4, :].bitcast(I32))
+            nc.scalar.dma_start(out=dst[0:P:8, :].bitcast(I32), in_=src[0].bitcast(I32))
 
         def load_weight(dst, src, h):
             rows = src.rearrange("(p j) c -> p j c", j=PACK)
@@ -59,13 +57,20 @@ def tile_attend_tcslotnorm_o_pl_kernel(
 
         w1_raw = [tile("w1_raw%d" % h, [P, PACK, R // 2], F32) for h in range(2)]
         dtab_w = tile("dtab_w", [P, T], U16)
-        load_weight(w1_raw, w1, 0)
         nc.sync.dma_start(offsets[:], offs)
+        load_weight(w1_raw, w1, 0)
         load_scales(tab_s, tab_scales)
+        load_scales(dtab_s, dtab_scales)
+        nc.scalar.activation(warm[:], exponent[:, 0:1], ACT.Silu)
         load_weight(w1_raw, w1, 1)
         nc.sync.dma_start(out=tab_w[:].bitcast(I32), in_=tab_words[0].bitcast(I32))
+
+        picked_s = tile("picked_s", [P, 2 * J], U8)
+        planes = tile("planes", [P, 2 * J], U8)
+        nc.vector.memset(planes[:].bitcast(I32), 0)
+        nc.vector.tensor_copy(picked_s[:, 0:J], tab_s[:].indirect(offsets[:]))
+        nc.vector.tensor_copy(picked_s[:, J : 2 * J], dtab_s[:].indirect(offsets[:]))
         nc.sync.dma_start(out=dtab_w[:].bitcast(I32), in_=dtab_words[0].bitcast(I32))
-        load_scales(dtab_s, dtab_scales)
         wor_raw = [tile("wor_raw%d" % h, [P, PACK, F // 2], F32) for h in range(2)]
         load_weight(wor_raw, wor, 0)
         load_weight(wor_raw, wor, 1)
@@ -90,14 +95,15 @@ def tile_attend_tcslotnorm_o_pl_kernel(
                 raw[h][:, :, PACK * lo : PACK * hi].rearrange("p j (m t) -> p m t j", t=PACK),
             )
 
-        x_s = gather("x_s", tab_s, U8)
 
         w1_bf = tile("w1_bf", [P, PACK, P, PACK], BF16)
         w1_q = tile("w1_q", [P, PACK, P], U32)
         w1_s = tile("w1_s", [P, PACK, P], U8)
-        deal(nc.scalar.copy, w1_bf, w1_raw, 0)
-        deal(nc.vector.tensor_copy, w1_bf, w1_raw, 1, 0, 44)
-        deal(nc.scalar.copy, w1_bf, w1_raw, 1, 44, 64)
+        deal(nc.scalar.copy, w1_bf, w1_raw, 0, 0, 32)
+        for r in range(4):
+            nc.scalar.dma_start(out=planes[r:P:32, :].bitcast(I32), in_=picked_s[8 * r : P : 32, :].bitcast(I32))
+        deal(nc.scalar.copy, w1_bf, w1_raw, 0, 32, 64)
+        deal(nc.vector.tensor_copy, w1_bf, w1_raw, 1)
         for t in range(PACK):
             nc.vector.quantize_mx(
                 out=w1_q[:, t, :].bitcast(FP8X4), scales=w1_s[:, t, :], in_=w1_bf[:, t, :, :].rearrange("p m j -> p (m j)")
@@ -111,17 +117,16 @@ def tile_attend_tcslotnorm_o_pl_kernel(
                     lhsT=w1_q[:, t, :].bitcast(FP8X4),
                     lhsT_scale=w1_s[:, t, :],
                     rhs=words[:].bitcast(FP4X4),
-                    rhs_scale=scales[:],
+                    rhs_scale=scales,
                     start=True,
                     stop=True,
                 )
             return banks
 
         x_w = gather("x_w", tab_w, U16)
-        a_ps = first_layer("a_ps", x_w, x_s)
+        a_ps = first_layer("a_ps", x_w, planes[:, 0:J])
         dx_w = gather("dx_w", dtab_w, U16)
-        dx_s = gather("dx_s", dtab_s, U8)
-        ta_ps = first_layer("ta_ps", dx_w, dx_s)
+        ta_ps = first_layer("ta_ps", dx_w, planes[:, J : 2 * J])
 
         a_sb = tile("a_sb", [P, PACK, J], F32)
         th = tile("th", [P, PACK, J], F32)
@@ -147,15 +152,13 @@ def tile_attend_tcslotnorm_o_pl_kernel(
             for t in range(2 * b, 2 * b + 2):
                 nc.scalar.copy(a_sb[:, t, :], a_ps[t][:])
 
-        wor_bf = tile("wor_bf", [P, PACK, P, PACK], BF16)
-        deal(nc.vector.tensor_copy, wor_bf, wor_raw, 0)
-        qinv = tile("qinv", [P, PACK], F32, tag="wor_raw0")
         for b in range(2):
             pair = slice(2 * b, 2 * b + 2)
-            nc.vector.reciprocal(qinv[:, pair], msq[:, pair])
+            qinv = tile("qinv%d" % b, [P, 2], F32)
+            nc.vector.reciprocal(qinv[:], msq[:, pair])
             for t in range(2 * b, 2 * b + 2):
                 nc.vector.scalar_tensor_tensor(
-                    u[:, t, :], ta_ps[t][:], qinv[:, t : t + 1], a_sb[:, t, :], ALU.mult, ALU.mult, accum_out=proj[:, t : t + 1]
+                    u[:, t, :], ta_ps[t][:], qinv[:, t % 2 : t % 2 + 1], a_sb[:, t, :], ALU.mult, ALU.mult, accum_out=proj[:, t : t + 1]
                 )
             for t in range(2 * b, 2 * b + 2):
                 nc.vector.scalar_tensor_tensor(
@@ -172,14 +175,15 @@ def tile_attend_tcslotnorm_o_pl_kernel(
                     right[:, t, :], ms[:, t, :], ACT.Identity, scale=scaled[:, 2, t : t + 1], bias=scaled[:, 3, t : t + 1]
                 )
 
+        wor_bf = tile("wor_bf", [P, PACK, P, PACK], BF16, tag="qinv0")
         wor_q = tile("wor_q", [P, PACK * P], U32)
         wor_s = tile("wor_s", [P, PACK * P], U8)
         for b in range(2):
             pair = slice(2 * b, 2 * b + 2)
             nc.vector.scalar_tensor_tensor(left[:, pair, :], th[:, pair, :], 1.0, u[:, pair, :], ALU.add, ALU.mult)
-        deal(nc.vector.tensor_copy, wor_bf, wor_raw, 1, 0, 32)
-        deal(nc.vector.tensor_copy, wor_bf, wor_raw, 1, 32, 64)
-        nc.vector.quantize_mx(out=wor_q[:].bitcast(FP8X4), scales=wor_s[:], in_=wor_bf[:].rearrange("p t m j -> p (t m j)"))
+        for h in range(2):
+            deal(nc.vector.tensor_copy, wor_bf, wor_raw, h, 0, 32)
+            deal(nc.vector.tensor_copy, wor_bf, wor_raw, h, 32, 64)
 
         def by_fours(ap):
             return ap.rearrange("p t (c i) -> p c t i", i=4)
@@ -198,6 +202,10 @@ def tile_attend_tcslotnorm_o_pl_kernel(
             fo_q = tile("fo_q%d" % h, [P, HALF], U32)
             fo_s = tile("fo_s%d" % h, [P, HALF], U8)
             nc.vector.tensor_tensor(woven(fo_bf[:]), by_fours(left[:, :, cols]), by_fours(right[:, :, cols]), ALU.mult)
+            if h == 0:
+                nc.vector.quantize_mx(
+                    out=wor_q[:].bitcast(FP8X4), scales=wor_s[:], in_=wor_bf[:].rearrange("p t m j -> p (t m j)")
+                )
             nc.vector.quantize_mx(out=fo_q[:].bitcast(FP8X4), scales=fo_s[:], in_=fo_bf[:].rearrange("p j t -> p (j t)"))
             bank = ps.tile([P, PACK, HALF], F32, name="y_ps%d" % h, tag="a_ps%d" % h)
             for t in range(PACK):

@@ -43,13 +43,15 @@ def tile_attend_tcslotnorm_o_pl_kernel(
         warm = tile("warm", [P, 1], F32)
 
         nc.vector.memset(tab_s[:].bitcast(I32), 0)
-        nc.vector.memset(dtab_s[:].bitcast(I32), 0)
         nc.vector.memset(exponent[:], -0.5)
+        nc.vector.memset(dtab_s[:].bitcast(I32), 0)
+        nc.scalar.activation(warm[:], exponent[:, 0:1], ACT.Silu)
         nc.gpsimd.dma_start(out=gain_sb[:], in_=gain.rearrange("(p t) o -> p (t o)", t=PACK))
         nc.gpsimd.dma_start(out=rs_sb[:], in_=rs.rearrange("(p t) o -> p (t o)", t=PACK))
 
         def load_scales(dst, src):
-            nc.scalar.dma_start(out=dst[0:P:8, :].bitcast(I32), in_=src[0].bitcast(I32))
+            for r in range(4):
+                nc.sync.dma_start(out=dst[r:P:32, :].bitcast(I32), in_=src[0, r:16:4, :].bitcast(I32))
 
         def load_weight(dst, src, h):
             rows = src.rearrange("(p j) c -> p j c", j=PACK)
@@ -57,20 +59,13 @@ def tile_attend_tcslotnorm_o_pl_kernel(
 
         w1_raw = [tile("w1_raw%d" % h, [P, PACK, R // 2], F32) for h in range(2)]
         dtab_w = tile("dtab_w", [P, T], U16)
-        nc.sync.dma_start(offsets[:], offs)
         load_weight(w1_raw, w1, 0)
+        nc.sync.dma_start(offsets[:], offs)
         load_scales(tab_s, tab_scales)
-        load_scales(dtab_s, dtab_scales)
-        nc.scalar.activation(warm[:], exponent[:, 0:1], ACT.Silu)
         load_weight(w1_raw, w1, 1)
         nc.sync.dma_start(out=tab_w[:].bitcast(I32), in_=tab_words[0].bitcast(I32))
-
-        picked_s = tile("picked_s", [P, 2 * J], U8)
-        planes = tile("planes", [P, 2 * J], U8)
-        nc.vector.memset(planes[:].bitcast(I32), 0)
-        nc.vector.tensor_copy(picked_s[:, 0:J], tab_s[:].indirect(offsets[:]))
-        nc.vector.tensor_copy(picked_s[:, J : 2 * J], dtab_s[:].indirect(offsets[:]))
         nc.sync.dma_start(out=dtab_w[:].bitcast(I32), in_=dtab_words[0].bitcast(I32))
+        load_scales(dtab_s, dtab_scales)
         wor_raw = [tile("wor_raw%d" % h, [P, PACK, F // 2], F32) for h in range(2)]
         load_weight(wor_raw, wor, 0)
         load_weight(wor_raw, wor, 1)
@@ -95,15 +90,14 @@ def tile_attend_tcslotnorm_o_pl_kernel(
                 raw[h][:, :, PACK * lo : PACK * hi].rearrange("p j (m t) -> p m t j", t=PACK),
             )
 
+        x_s = gather("x_s", tab_s, U8)
 
         w1_bf = tile("w1_bf", [P, PACK, P, PACK], BF16)
         w1_q = tile("w1_q", [P, PACK, P], U32)
         w1_s = tile("w1_s", [P, PACK, P], U8)
-        deal(nc.scalar.copy, w1_bf, w1_raw, 0, 0, 32)
-        for r in range(4):
-            nc.scalar.dma_start(out=planes[r:P:32, :].bitcast(I32), in_=picked_s[8 * r : P : 32, :].bitcast(I32))
-        deal(nc.scalar.copy, w1_bf, w1_raw, 0, 32, 64)
-        deal(nc.vector.tensor_copy, w1_bf, w1_raw, 1)
+        deal(nc.scalar.copy, w1_bf, w1_raw, 0)
+        deal(nc.vector.tensor_copy, w1_bf, w1_raw, 1, 0, 44)
+        deal(nc.scalar.copy, w1_bf, w1_raw, 1, 44, 64)
         for t in range(PACK):
             nc.vector.quantize_mx(
                 out=w1_q[:, t, :].bitcast(FP8X4), scales=w1_s[:, t, :], in_=w1_bf[:, t, :, :].rearrange("p m j -> p (m j)")
@@ -117,16 +111,17 @@ def tile_attend_tcslotnorm_o_pl_kernel(
                     lhsT=w1_q[:, t, :].bitcast(FP8X4),
                     lhsT_scale=w1_s[:, t, :],
                     rhs=words[:].bitcast(FP4X4),
-                    rhs_scale=scales,
+                    rhs_scale=scales[:],
                     start=True,
                     stop=True,
                 )
             return banks
 
         x_w = gather("x_w", tab_w, U16)
-        a_ps = first_layer("a_ps", x_w, planes[:, 0:J])
+        a_ps = first_layer("a_ps", x_w, x_s)
         dx_w = gather("dx_w", dtab_w, U16)
-        ta_ps = first_layer("ta_ps", dx_w, planes[:, J : 2 * J])
+        dx_s = gather("dx_s", dtab_s, U8)
+        ta_ps = first_layer("ta_ps", dx_w, dx_s)
 
         a_sb = tile("a_sb", [P, PACK, J], F32)
         th = tile("th", [P, PACK, J], F32)
@@ -152,9 +147,11 @@ def tile_attend_tcslotnorm_o_pl_kernel(
             for t in range(2 * b, 2 * b + 2):
                 nc.scalar.copy(a_sb[:, t, :], a_ps[t][:])
 
+        wor_bf = tile("wor_bf", [P, PACK, P, PACK], BF16)
+        deal(nc.vector.tensor_copy, wor_bf, wor_raw, 0)
         for b in range(2):
             pair = slice(2 * b, 2 * b + 2)
-            qinv = tile("qinv%d" % b, [P, 2], F32)
+            qinv = tile("qinv%d" % b, [P, 2], F32, tag="wor_raw0")
             nc.vector.reciprocal(qinv[:], msq[:, pair])
             for t in range(2 * b, 2 * b + 2):
                 nc.vector.scalar_tensor_tensor(
@@ -165,25 +162,23 @@ def tile_attend_tcslotnorm_o_pl_kernel(
                     u[:, t, :], a_sb[:, t, :], proj[:, t : t + 1], ta_ps[t][:], ALU.mult, ALU.subtract
                 )
 
-        for b in range(2):
-            for t in range(2 * b, 2 * b + 2):
-                nc.scalar.activation(th[:, t, :], a_sb[:, t, :], ACT.Tanh, scale=scaled[:, 0, t : t + 1])
-            for t in range(2 * b, 2 * b + 2):
-                nc.scalar.activation(ms[:, t, :], a_sb[:, t, :], ACT.Silu, scale=scaled[:, 1, t : t + 1])
-            for t in range(2 * b, 2 * b + 2):
+        def gate(tiles, cols):
+            for t in tiles:
+                nc.scalar.activation(th[:, t, cols], a_sb[:, t, cols], ACT.Tanh, scale=scaled[:, 0, t : t + 1])
+            for t in tiles:
+                nc.scalar.activation(ms[:, t, cols], a_sb[:, t, cols], ACT.Silu, scale=scaled[:, 1, t : t + 1])
+            for t in tiles:
                 nc.scalar.activation(
-                    right[:, t, :], ms[:, t, :], ACT.Identity, scale=scaled[:, 2, t : t + 1], bias=scaled[:, 3, t : t + 1]
+                    right[:, t, cols], ms[:, t, cols], ACT.Identity, scale=scaled[:, 2, t : t + 1], bias=scaled[:, 3, t : t + 1]
                 )
+            pair = slice(tiles[0], tiles[-1] + 1)
+            nc.vector.scalar_tensor_tensor(left[:, pair, cols], th[:, pair, cols], 1.0, u[:, pair, cols], ALU.add, ALU.mult)
 
-        wor_bf = tile("wor_bf", [P, PACK, P, PACK], BF16, tag="qinv0")
         wor_q = tile("wor_q", [P, PACK * P], U32)
         wor_s = tile("wor_s", [P, PACK * P], U8)
-        for b in range(2):
-            pair = slice(2 * b, 2 * b + 2)
-            nc.vector.scalar_tensor_tensor(left[:, pair, :], th[:, pair, :], 1.0, u[:, pair, :], ALU.add, ALU.mult)
-        for h in range(2):
-            deal(nc.vector.tensor_copy, wor_bf, wor_raw, h, 0, 32)
-            deal(nc.vector.tensor_copy, wor_bf, wor_raw, h, 32, 64)
+        gate((0, 1), slice(0, J))
+        deal(nc.vector.tensor_copy, wor_bf, wor_raw, 1, 0, 32)
+        deal(nc.vector.tensor_copy, wor_bf, wor_raw, 1, 32, 64)
 
         def by_fours(ap):
             return ap.rearrange("p t (c i) -> p c t i", i=4)
@@ -194,13 +189,13 @@ def tile_attend_tcslotnorm_o_pl_kernel(
         y_q = tile("y_q", [P, J], U32)
         y_s = tile("y_s", [P, J], U8)
         y_rows = out_0.rearrange("(p t) j -> p t j", t=PACK)
-        y_words = out_1[0].rearrange("p c r -> p (c r)").bitcast(I32)
         y_ps = []
         for h in range(2):
             cols = slice(h * HALF, (h + 1) * HALF)
             fo_bf = tile("fo_bf%d" % h, [P, HALF, PACK], BF16)
             fo_q = tile("fo_q%d" % h, [P, HALF], U32)
             fo_s = tile("fo_s%d" % h, [P, HALF], U8)
+            gate((2, 3), cols)
             nc.vector.tensor_tensor(woven(fo_bf[:]), by_fours(left[:, :, cols]), by_fours(right[:, :, cols]), ALU.mult)
             if h == 0:
                 nc.vector.quantize_mx(
@@ -223,16 +218,14 @@ def tile_attend_tcslotnorm_o_pl_kernel(
             cols = slice(h * HALF, (h + 1) * HALF)
             y = tile("y%d" % h, [P, PACK, HALF], F32)
             y_bf = tile("y_bf%d" % h, [P, HALF, PACK], BF16)
-            if h == 1:
-                nc.vector.tensor_tensor(woven(y_bf[:]), by_fours(y_ps[h][:]), by_fours(res_sb[:, :, cols]), ALU.add)
             nc.vector.tensor_tensor(y[:], y_ps[h][:], res_sb[:, :, cols], ALU.add)
             nc.sync.dma_start(out=y_rows[:, :, cols], in_=y[:])
-            if h == 0:
-                nc.scalar.copy(woven(y_bf[:]), by_fours(y[:]))
+            copy = nc.scalar.copy if h == 0 else nc.vector.tensor_copy
+            copy(woven(y_bf[:]), by_fours(y[:]))
             nc.vector.quantize_mx(
                 out=y_q[:, cols].bitcast(FP8X4), scales=y_s[:, cols], in_=y_bf[:].rearrange("p j t -> p (j t)")
             )
-            nc.scalar.dma_start(out=y_words[:, cols], in_=y_q[:, cols].bitcast(I32))
+        nc.sync.dma_start(out=out_1[0].rearrange("p c r -> p (c r)").bitcast(I32), in_=y_q[:].bitcast(I32))
         for r in range(4):
-            queue = nc.sync if r % 2 == 0 else nc.scalar
+            queue = nc.scalar if r % 2 == 0 else nc.sync
             queue.dma_start(out=out_2[0, r:16:4, :].bitcast(I32), in_=y_s[r:P:32, :].bitcast(I32))

from contextlib import ExitStack

import concourse.mybir as mybir

K, R, F, T, J = 512, 512, 512, 2048, 256
FLOPS = 2 * (2 * K * R * J + R * F * J)

F32 = mybir.dt.float32
BF16 = mybir.dt.bfloat16
I32 = mybir.dt.int32
U32 = mybir.dt.uint32
U16 = mybir.dt.uint16
U8 = mybir.dt.uint8
FP8X4 = mybir.dt.float8_e4m3fn_x4
FP4X4 = mybir.dt.float4_e2m1fn_x4
ACT = mybir.ActivationFunctionType
ALU = mybir.AluOpType

P = 128
PACK = 4
HALF = J // 2
EPS = 0.01


def tile_attend_tcslotnorm_o_pl_kernel(
    tc, tab_words, tab_scales, dtab_words, dtab_scales, w1, gain, rs, wor, res, offs, out_0, out_1, out_2
):
    nc = tc.nc
    with ExitStack() as ctx:
        sb = ctx.enter_context(tc.tile_pool(name="sb", bufs=1))
        ps = ctx.enter_context(tc.psum_pool(name="ps", bufs=1))

        def tile(name, shape, dtype, tag=None):
            return sb.tile(shape, dtype, name=name, tag=tag or name, align_bytes=64)

        offsets = sb.tile([P, J // 16], U16, name="offsets")
        tab_w = tile("tab_w", [P, T], U16)
        tab_s = tile("tab_s", [P, T], U8)
        dtab_s = tile("dtab_s", [P, T], U8)
        gain_sb = tile("gain_sb", [P, PACK], F32)
        rs_sb = tile("rs_sb", [P, PACK], F32)
        exponent = tile("exponent", [P, PACK], F32)
        warm = tile("warm", [P, 1], F32)

        nc.vector.memset(tab_s[:].bitcast(I32), 0)
        nc.vector.memset(exponent[:], -0.5)
        nc.vector.memset(dtab_s[:].bitcast(I32), 0)
        nc.scalar.activation(warm[:], exponent[:, 0:1], ACT.Silu)
        nc.gpsimd.dma_start(out=gain_sb[:], in_=gain.rearrange("(p t) o -> p (t o)", t=PACK))
        nc.gpsimd.dma_start(out=rs_sb[:], in_=rs.rearrange("(p t) o -> p (t o)", t=PACK))

        def load_scales(dst, src):
            for r in range(4):
                nc.sync.dma_start(out=dst[r:P:32, :].bitcast(I32), in_=src[0, r:16:4, :].bitcast(I32))

        def load_weight(dst, src, h):
            rows = src.rearrange("(p j) c -> p j c", j=PACK)
            nc.sync.dma_start(out=dst[h][:], in_=rows[:, :, h * 256 : (h + 1) * 256])

        w1_raw = [tile("w1_raw%d" % h, [P, PACK, R // 2], F32) for h in range(2)]
        dtab_w = tile("dtab_w", [P, T], U16)
        load_weight(w1_raw, w1, 0)
        nc.sync.dma_start(offsets[:], offs)
        load_scales(tab_s, tab_scales)
        load_weight(w1_raw, w1, 1)
        nc.sync.dma_start(out=tab_w[:].bitcast(I32), in_=tab_words[0].bitcast(I32))
        nc.sync.dma_start(out=dtab_w[:].bitcast(I32), in_=dtab_words[0].bitcast(I32))
        load_scales(dtab_s, dtab_scales)
        wor_raw = [tile("wor_raw%d" % h, [P, PACK, F // 2], F32) for h in range(2)]
        load_weight(wor_raw, wor, 0)
        load_weight(wor_raw, wor, 1)
        res_sb = tile("res_sb", [P, PACK, J], F32)
        nc.sync.dma_start(out=res_sb[:], in_=res.rearrange("(p t) j -> p t j", t=PACK))

        root = float(J) ** 0.5
        coef = tile("coef", [P, 4, PACK], F32)
        nc.gpsimd.tensor_scalar(coef[:, 0, :], gain_sb[:], 0.5 * root, 0.0, ALU.mult, ALU.add)
        nc.gpsimd.tensor_scalar(coef[:, 1, :], gain_sb[:], -root, 0.0, ALU.mult, ALU.add)
        nc.gpsimd.tensor_tensor(coef[:, 2, :], coef[:, 0, :], rs_sb[:], ALU.mult)
        nc.gpsimd.tensor_scalar(coef[:, 3, :], coef[:, 2, :], -1.0, 0.0, ALU.mult, ALU.add)

        def gather(name, window, dtype):
            picked = tile(name, [P, J], dtype)
            nc.vector.tensor_copy(picked[:], window[:].indirect(offsets[:]))
            return picked

        def deal(copy, grouped, raw, h, lo=0, hi=64):
            copy(
                grouped[:, :, h * 64 + lo : h * 64 + hi, :].rearrange("p t m j -> p m t j"),
                raw[h][:, :, PACK * lo : PACK * hi].rearrange("p j (m t) -> p m t j", t=PACK),
            )

        x_s = gather("x_s", tab_s, U8)

        w1_bf = tile("w1_bf", [P, PACK, P, PACK], BF16)
        w1_q = tile("w1_q", [P, PACK, P], U32)
        w1_s = tile("w1_s", [P, PACK, P], U8)
        deal(nc.scalar.copy, w1_bf, w1_raw, 0)
        deal(nc.vector.tensor_copy, w1_bf, w1_raw, 1, 0, 44)
        deal(nc.scalar.copy, w1_bf, w1_raw, 1, 44, 64)
        for t in range(PACK):
            nc.vector.quantize_mx(
                out=w1_q[:, t, :].bitcast(FP8X4), scales=w1_s[:, t, :], in_=w1_bf[:, t, :, :].rearrange("p m j -> p (m j)")
            )

        def first_layer(name, words, scales):
            banks = [ps.tile([P, J], F32, name="%s%d" % (name, t)) for t in range(PACK)]
            for t in range(PACK):
                nc.tensor.matmul_mx(
                    out=banks[t][:],
                    lhsT=w1_q[:, t, :].bitcast(FP8X4),
                    lhsT_scale=w1_s[:, t, :],
                    rhs=words[:].bitcast(FP4X4),
                    rhs_scale=scales[:],
                    start=True,
                    stop=True,
                )
            return banks

        x_w = gather("x_w", tab_w, U16)
        a_ps = first_layer("a_ps", x_w, x_s)
        dx_w = gather("dx_w", dtab_w, U16)
        dx_s = gather("dx_s", dtab_s, U8)
        ta_ps = first_layer("ta_ps", dx_w, dx_s)

        a_sb = tile("a_sb", [P, PACK, J], F32)
        th = tile("th", [P, PACK, J], F32)
        ms = tile("ms", [P, PACK, J], F32)
        u = tile("u", [P, PACK, J], F32)
        left = tile("left", [P, PACK, J], F32)
        right = tile("right", [P, PACK, J], F32)
        ssq = tile("ssq", [P, PACK], F32)
        msq = tile("msq", [P, PACK], F32)
        rinv = tile("rinv", [P, PACK], F32)
        scaled = tile("scaled", [P, 4, PACK], F32)
        proj = tile("proj", [P, PACK], F32)

        for b in range(2):
            pair = slice(2 * b, 2 * b + 2)
            for t in range(2 * b, 2 * b + 2):
                nc.scalar.activation(th[:, t, :], a_ps[t][:], ACT.Square, accum_out=ssq[:, t : t + 1])
            nc.gpsimd.tensor_scalar(msq[:, pair], ssq[:, pair], EPS * J, 1.0, ALU.add, ALU.mult)
            nc.gpsimd.tensor_tensor(rinv[:, pair], msq[:, pair], exponent[:, pair], ALU.pow)
            nc.gpsimd.tensor_tensor(
                scaled[:, :, pair], coef[:, :, pair], rinv[:, pair].unsqueeze(1).to_broadcast([P, 4, 2]), ALU.mult
            )
            for t in range(2 * b, 2 * b + 2):
                nc.scalar.copy(a_sb[:, t, :], a_ps[t][:])

        wor_bf = tile("wor_bf", [P, PACK, P, PACK], BF16)
        deal(nc.vector.tensor_copy, wor_bf, wor_raw, 0)
        for b in range(2):
            pair = slice(2 * b, 2 * b + 2)
            qinv = tile("qinv%d" % b, [P, 2], F32, tag="wor_raw0")
            nc.vector.reciprocal(qinv[:], msq[:, pair])
            for t in range(2 * b, 2 * b + 2):
                nc.vector.scalar_tensor_tensor(
                    u[:, t, :], ta_ps[t][:], qinv[:, t % 2 : t % 2 + 1], a_sb[:, t, :], ALU.mult, ALU.mult, accum_out=proj[:, t : t + 1]
                )
            for t in range(2 * b, 2 * b + 2):
                nc.vector.scalar_tensor_tensor(
                    u[:, t, :], a_sb[:, t, :], proj[:, t : t + 1], ta_ps[t][:], ALU.mult, ALU.subtract
                )

        def gate(tiles, cols):
            for t in tiles:
                nc.scalar.activation(th[:, t, cols], a_sb[:, t, cols], ACT.Tanh, scale=scaled[:, 0, t : t + 1])
            for t in tiles:
                nc.scalar.activation(ms[:, t, cols], a_sb[:, t, cols], ACT.Silu, scale=scaled[:, 1, t : t + 1])
            for t in tiles:
                nc.scalar.activation(
                    right[:, t, cols], ms[:, t, cols], ACT.Identity, scale=scaled[:, 2, t : t + 1], bias=scaled[:, 3, t : t + 1]
                )
            pair = slice(tiles[0], tiles[-1] + 1)
            nc.vector.scalar_tensor_tensor(left[:, pair, cols], th[:, pair, cols], 1.0, u[:, pair, cols], ALU.add, ALU.mult)

        wor_q = tile("wor_q", [P, PACK * P], U32)
        wor_s = tile("wor_s", [P, PACK * P], U8)
        gate((0, 1), slice(0, J))
        deal(nc.vector.tensor_copy, wor_bf, wor_raw, 1, 0, 32)
        deal(nc.vector.tensor_copy, wor_bf, wor_raw, 1, 32, 64)

        def by_fours(ap):
            return ap.rearrange("p t (c i) -> p c t i", i=4)

        def woven(ap):
            return ap.rearrange("p (c i) t -> p c t i", i=4)

        y_q = tile("y_q", [P, J], U32)
        y_s = tile("y_s", [P, J], U8)
        y_rows = out_0.rearrange("(p t) j -> p t j", t=PACK)
        y_ps = []
        for h in range(2):
            cols = slice(h * HALF, (h + 1) * HALF)
            fo_bf = tile("fo_bf%d" % h, [P, HALF, PACK], BF16)
            fo_q = tile("fo_q%d" % h, [P, HALF], U32)
            fo_s = tile("fo_s%d" % h, [P, HALF], U8)
            gate((2, 3), cols)
            nc.vector.tensor_tensor(woven(fo_bf[:]), by_fours(left[:, :, cols]), by_fours(right[:, :, cols]), ALU.mult)
            if h == 0:
                nc.vector.quantize_mx(
                    out=wor_q[:].bitcast(FP8X4), scales=wor_s[:], in_=wor_bf[:].rearrange("p t m j -> p (t m j)")
                )
            nc.vector.quantize_mx(out=fo_q[:].bitcast(FP8X4), scales=fo_s[:], in_=fo_bf[:].rearrange("p j t -> p (j t)"))
            bank = ps.tile([P, PACK, HALF], F32, name="y_ps%d" % h, tag="a_ps%d" % h)
            for t in range(PACK):
                nc.tensor.matmul_mx(
                    out=bank[:, t, :],
                    lhsT=wor_q[:, t * P : (t + 1) * P].bitcast(FP8X4),
                    lhsT_scale=wor_s[:, t * P : (t + 1) * P],
                    rhs=fo_q[:].bitcast(FP8X4),
                    rhs_scale=fo_s[:],
                    start=True,
                    stop=True,
                )
            y_ps.append(bank)
        for h in range(2):
            cols = slice(h * HALF, (h + 1) * HALF)
            y = tile("y%d" % h, [P, PACK, HALF], F32)
            y_bf = tile("y_bf%d" % h, [P, HALF, PACK], BF16)
            nc.vector.tensor_tensor(y[:], y_ps[h][:], res_sb[:, :, cols], ALU.add)
            nc.sync.dma_start(out=y_rows[:, :, cols], in_=y[:])
            copy = nc.scalar.copy if h == 0 else nc.vector.tensor_copy
            copy(woven(y_bf[:]), by_fours(y[:]))
            nc.vector.quantize_mx(
                out=y_q[:, cols].bitcast(FP8X4), scales=y_s[:, cols], in_=y_bf[:].rearrange("p j t -> p (j t)")
            )
        nc.sync.dma_start(out=out_1[0].rearrange("p c r -> p (c r)").bitcast(I32), in_=y_q[:].bitcast(I32))
        for r in range(4):
            queue = nc.scalar if r % 2 == 0 else nc.sync
            queue.dma_start(out=out_2[0, r:16:4, :].bitcast(I32), in_=y_s[r:P:32, :].bitcast(I32))
